import numpy as np, ml_dtypes
CORES = [24,40,56,80,88,96]
N = 6
import mx_ref
NC, G = 256, 4
EPS = 0.001
BF = ml_dtypes.bfloat16
def cut(t, i, w=512):
    return t[:, w * i:w * i + w]
def tile(rs):
    return np.stack(rs, axis=2).reshape(128, -1).astype(BF)
def layer(w, X):
    out = []
    for i in range(G):
        for t in range(len(X)):
            p = mx_ref.matmul(mx_ref.quantize(cut(w, len(X) * i + t)), X[t])
            z = p if t == 0 else z + p
        out.append(z)
    return out
def setup_inputs(rng):
    def f(*shape):
        return mx_ref.flush((rng.standard_normal(shape, dtype=np.float32) * np.exp2(rng.integers(-2, 3, shape[:-1] + (1,)))).astype(BF))
    return {"x": f(N, 128, 4 * NC), "w1": f(N, 128, G * 512), "w2": f(N, 128, 2 * 512)}
def setup_inputs_blocks(rng):
    d = setup_inputs(rng)
    for k in ("x", "w1", "w2"): d[k] = mx_ref.spread(d[k], rng, 4)
    return d
def setup_inputs_wide(rng):
    d = setup_inputs(rng)
    for k in ("x", "w1", "w2"): d[k] = mx_ref.flush((d[k].astype(np.float32) * np.exp2(rng.integers(-6, 7, (N, 1, 1))).astype(np.float32)).astype(BF))
    return d
def setup_inputs_cols(rng):
    d = setup_inputs(rng); v = d["x"].astype(np.float32).reshape(N, 128, -1, 4)
    d["x"] = mx_ref.flush((v * np.exp2(rng.integers(-6, 7, (N, 1, v.shape[2], 1))).astype(np.float32)).reshape(d["x"].shape).astype(BF))
    return d
def setup_inputs_faint(rng):
    d = setup_inputs(rng); d["x"] = mx_ref.flush((d["x"].astype(np.float32) * np.float32(2.0 ** -12)).astype(BF))
    return d
def reference(x, w1, w2, own=None):
    h = np.zeros((N, 128, 4 * NC), BF)
    for r in range(N):
        Z = layer(w1[r], [mx_ref.quantize(x[r])]); R = Z
        ms = sum((v.astype(np.float64) ** 2).sum(axis=0) for v in R) / 512
        s = (1 / np.sqrt(ms + EPS)).astype(np.float32)
        h[r] = tile([v * s for v in R])
    use = h if own is None else own["h"]
    H = [mx_ref.quantize(use[j]) for j in range(N)]
    y = np.zeros((N, 128, NC), np.float32)
    for r in range(N):
        y[r] = mx_ref.matmul(mx_ref.quantize(cut(w2[r], 0)), H[r]) + mx_ref.matmul(mx_ref.quantize(cut(w2[r], 1)), H[(r + 1) % N])
    return {"h": h, "y": y}

@@ -1,0 +1,241 @@
+from concourse.mybir import dt, AluOpType, ActivationFunctionType
+
+NCH = 2
+CW = 128
+G = 4
+EPS = 0.001
+ROWS = 512
+
+SCRATCH = {
+    "xt": ("sbuf", [128, 1024], "bfloat16"),
+    "w1t": ("sbuf", [128, 2048], "bfloat16"),
+    "w2t": ("sbuf", [128, 1024], "bfloat16"),
+    "xq": ("sbuf", [128, 256], "float8_e4m3fn_x4"), "xs": ("sbuf", [128, 256], "uint8"),
+    "w1q": ("sbuf", [128, 512], "float8_e4m3fn_x4"), "w1s": ("sbuf", [128, 512], "uint8"),
+    "w2q": ("sbuf", [128, 256], "float8_e4m3fn_x4"), "w2s": ("sbuf", [128, 256], "uint8"),
+    "ht": ("sbuf", [128, 1024], "bfloat16"),
+    "hq": ("sbuf", [128, 256], "float8_e4m3fn_x4"), "hs": ("sbuf", [128, 256], "uint8"),
+    "rq": ("sbuf", [128, 256], "float8_e4m3fn_x4"), "rs": ("sbuf", [128, 256], "uint8"),
+    "sq": ("sbuf", [128, 1024], "float32"),
+    "zs": ("sbuf", [128, 1024], "float32"),
+    "ones": ("sbuf", [128, 128], "float32"),
+    "ident": ("sbuf", [128, 128], "float32"),
+    "cinv": ("sbuf", [128, 4], "float32"),
+    "ceps": ("sbuf", [128, 4], "float32"),
+    "rcol": ("sbuf", [128, 8], "float32"),
+    "dg": ("sbuf", [128, 256], "float32"),
+    "yt": ("sbuf", [128, 256], "float32"),
+    "ps": ("psum", [128, 4096], "float32"),
+}
+
+SEMAPHORES = (
+    ["lx0", "lx1", "lw2", "on", "cs", "idn", "qx0", "qx1", "qw2", "sent", "sh"]
+    + ["lw1_%d" % b for b in range(G)] + ["qw1_%d" % b for b in range(G)]
+    + ["%s%d%d" % (n, c, b) for n in ("mx", "sq", "cp") for c in range(NCH) for b in range(G)]
+    + ["%s%d" % (n, c) for n in ("st", "r", "d", "bc", "mu", "qh", "arr", "y", "yc", "sy") for c in range(NCH)]
+)
+
+
+def _engines(mask):
+    return bin(mask).count("1")
+
+
+def _route(T, topo, s):
+    n = len(T.cores)
+    src, dst = T.cores[s], T.cores[(s - 1) % n]
+    if topo.may_write(src, dst):
+        return src, dst, src, src
+    helpers = [k for k in range(topo.CORES_PER_CHIP * topo.CHIPS)
+               if topo.chip(k) == topo.chip(src) and topo.die(k) == topo.die(src)
+               and T.rank_of(k) is None and topo.may_write(k, dst)]
+    return src, dst, helpers[0], helpers[1]
+
+
+def _send(g, T, topo, src, dst, out_ap, in_ap, sem):
+    rid, pid, _ = topo.addr(dst)
+    m = topo.mask(src, dst)
+    g.remote_dma(out_ap=out_ap, in_ap=in_ap, remote_sem=sem, local_sem=T.sem.sent,
+                 pid=pid, routing_id=rid, dma_engine_mask=m)
+    return _engines(m)
+
+
+def _codes(buf, c):
+    return buf[:, CW * c:CW * c + CW].bitcast(dt.uint8)
+
+
+def _plane(buf, c):
+    return buf[:, CW * c:CW * c + CW]
+
+
+def _helper_program(g, core, T, topo):
+    for s in range(len(T.cores)):
+        src, dst, via_q, via_s = _route(T, topo, s)
+        if core == src or core not in (via_q, via_s):
+            continue
+        got = _engines(topo.mask(src, core))
+        left = 0
+        for c in range(NCH):
+            g.wait_ge(T.sem["arr%d" % c], got)
+            if core == via_q:
+                left += _send(g, T, topo, core, dst, _codes(T.rq, c), _codes(T.rq, c), T.sem["arr%d" % c])
+            else:
+                left += _send(g, T, topo, core, dst, _plane(T.rs, c), _plane(T.rs, c), T.sem["arr%d" % c])
+        g.wait_ge(T.sem.sent, left)
+
+
+def rank_program(g, core, T, topo):
+    rank = T.rank_of(core)
+    if rank is None:
+        _helper_program(g, core, T, topo)
+        return
+    S = T.sem
+    n = len(T.cores)
+    V, A, P, Y = g.vector, g.scalar, g.tensor, g.sync
+    mult = AluOpType.mult
+    Act = ActivationFunctionType
+
+    def bank(k, a=0, b=CW):
+        return T.ps[:, 512 * k + a:512 * k + b]
+
+    def z(c, b):
+        return bank(G * c + b)
+
+    def piece(buf, c, b):
+        return buf[:, 512 * c + CW * b:512 * c + CW * b + CW]
+
+    stat = [bank(7, 128, 129), bank(3, 128, 129)]
+    spread = [bank(0), bank(4)]
+    ybank = [bank(1), bank(2)]
+
+    Y.dma_start(T.xt[:, 0:512], T.x[:, 0:512]).then_inc(S.lx0, 16)
+    A.dma_start(T.w1t[:, 0:512], T.w1[:, 0:512]).then_inc(S.lw1_0, 16)
+    Y.dma_start(T.w1t[:, 512:1024], T.w1[:, 512:1024]).then_inc(S.lw1_1, 16)
+    A.dma_start(T.w1t[:, 1024:1536], T.w1[:, 1024:1536]).then_inc(S.lw1_2, 16)
+    Y.dma_start(T.w1t[:, 1536:2048], T.w1[:, 1536:2048]).then_inc(S.lw1_3, 16)
+    Y.dma_start(T.xt[:, 512:1024], T.x[:, 512:1024]).then_inc(S.lx1, 16)
+    Y.wait_ge(S.lx0, 16)
+    Y.dma_start(T.w2t[:], T.w2[:]).then_inc(S.lw2, 16)
+
+    V.memset(T.ones[:], 1.0).then_inc(S.on, 1)
+    V.memset(T.cinv[:], 1.0 / ROWS).then_inc(S.cs, 1)
+    V.memset(T.ceps[:], EPS / 128.0).then_inc(S.cs, 1)
+    g.wait_ge(S.on, 1)
+    g.affine_select(T.ident[:], T.ones[:], [[-1, 128]], AluOpType.is_equal, 0.0, 0, 1).then_inc(S.idn, 1)
+
+    V.wait_ge(S.lx0, 16)
+    V.quantize_mx(T.xq[:, 0:CW], T.xs[:, 0:CW], T.xt[:, 0:512]).then_inc(S.qx0, 1)
+    for b in range(G):
+        V.wait_ge(S["lw1_%d" % b], 16)
+        V.quantize_mx(T.w1q[:, CW * b:CW * b + CW], T.w1s[:, CW * b:CW * b + CW],
+                      T.w1t[:, 512 * b:512 * b + 512]).then_inc(S["qw1_%d" % b], 1)
+    V.wait_ge(S.st0, 1)
+    V.reciprocal(T.rcol[:, 0:1], stat[0]).then_inc(S.r0, 1)
+    V.wait_ge(S.lx1, 16)
+    V.quantize_mx(T.xq[:, CW:2 * CW], T.xs[:, CW:2 * CW], T.xt[:, 512:1024]).then_inc(S.qx1, 1)
+    for b in range(G):
+        V.wait_ge(S["mx1%d" % b], 1)
+        V.tensor_copy(piece(T.zs, 1, b), z(1, b)).then_inc(S["cp1%d" % b], 1)
+        V.wait_ge(S["cp1%d" % b], 1)
+        V.tensor_tensor(piece(T.sq, 1, b), z(1, b), piece(T.zs, 1, b), mult).then_inc(S["sq1%d" % b], 1)
+    V.wait_ge(S.st1, 1)
+    V.reciprocal(T.rcol[:, 4:5], stat[1]).then_inc(S.r1, 1)
+    for c in range(NCH):
+        V.wait_ge(S["bc%d" % c], 1)
+        for b in range(G):
+            V.wait_ge(S["cp%d%d" % (c, b)], 1)
+            V.tensor_tensor(T.ht[:, 512 * c + b:512 * c + 512:4], piece(T.zs, c, b), spread[c], mult
+                            ).then_inc(S["mu%d" % c], 1)
+        V.wait_ge(S["mu%d" % c], G)
+        V.quantize_mx(T.hq[:, CW * c:CW * c + CW], T.hs[:, CW * c:CW * c + CW],
+                      T.ht[:, 512 * c:512 * c + 512]).then_inc(S["qh%d" % c], 1)
+    V.wait_ge(S.lw2, 16)
+    V.quantize_mx(T.w2q[:], T.w2s[:], T.w2t[:]).then_inc(S.qw2, 1)
+    for c in range(NCH):
+        V.wait_ge(S["y%d" % c], 1)
+        V.tensor_copy(T.yt[:, CW * c:CW * c + CW], ybank[c]).then_inc(S["yc%d" % c], 1)
+
+    for b in range(G):
+        A.wait_ge(S["mx0%d" % b], 1)
+        A.activation(piece(T.sq, 0, b), z(0, b), Act.Square).then_inc(S["sq0%d" % b], 1)
+    for b in range(G):
+        A.activation(piece(T.zs, 0, b), z(0, b), Act.Copy).then_inc(S["cp0%d" % b], 1)
+    A.wait_ge(S.idn, 1)
+    for c in range(NCH):
+        A.wait_ge(S["r%d" % c], 1)
+        A.activation(T.dg[:, CW * c:CW * c + CW], T.ident[:], Act.Sqrt,
+                     scale=T.rcol[:, 4 * c:4 * c + 1]).then_inc(S["d%d" % c], 1)
+
+    def layer1(c, b):
+        P.matmul_mx(z(c, b), T.w1q[:, CW * b:CW * b + CW], T.w1s[:, CW * b:CW * b + CW],
+                    T.xq[:, CW * c:CW * c + CW], T.xs[:, CW * c:CW * c + CW], True, True).then_inc(S["mx%d%d" % (c, b)], 1)
+
+    def mean(c, b):
+        P.wait_ge(S["sq%d%d" % (c, b)], 1)
+        i = P.matmul(stat[c], piece(T.sq, c, b), T.cinv[:, 0:1], False, b == G - 1)
+        if b == G - 1:
+            i.then_inc(S["st%d" % c], 1)
+
+    P.wait_ge(S.on, 1)
+    P.wait_ge(S.cs, 2)
+    P.matmul(stat[0], T.ones[:], T.ceps[:, 0:1], True, False)
+    P.wait_ge(S.qx0, 1)
+    P.wait_ge(S.qw1_0, 1)
+    layer1(0, 0)
+    P.wait_ge(S.qw1_1, 1)
+    layer1(0, 1)
+    mean(0, 0)
+    P.wait_ge(S.qw1_2, 1)
+    layer1(0, 2)
+    mean(0, 1)
+    P.wait_ge(S.qw1_3, 1)
+    layer1(0, 3)
+    mean(0, 2)
+    mean(0, 3)
+    P.wait_ge(S.qx1, 1)
+    layer1(1, 0)
+    layer1(1, 1)
+    layer1(1, 2)
+    P.wait_ge(S.r0, 1)
+    layer1(1, 3)
+    P.wait_ge(S.cp03, 1)
+    P.matmul(stat[1], T.ones[:], T.ceps[:, 0:1], True, False)
+    for b in range(G):
+        mean(1, b)
+    P.wait_ge(S.cp00, 1)
+    for c in range(NCH):
+        P.wait_ge(S["d%d" % c], 1)
+        P.matmul(spread[c], T.ones[:], T.dg[:, CW * c:CW * c + CW], True, True).then_inc(S["bc%d" % c], 1)
+    P.wait_ge(S.qw2, 1)
+    P.wait_ge(S.cp01, 1)
+    P.wait_ge(S.cp02, 1)
+    for c in range(NCH):
+        P.wait_ge(S["qh%d" % c], 1)
+        P.matmul_mx(ybank[c], T.w2q[:, 0:CW], T.w2s[:, 0:CW],
+                    T.hq[:, CW * c:CW * c + CW], T.hs[:, CW * c:CW * c + CW], True, False)
+    _, _, in_q, in_s = _route(T, topo, (rank + 1) % n)
+    landed = _engines(topo.mask(in_q, core)) + _engines(topo.mask(in_s, core))
+    for c in range(NCH):
+        P.wait_ge(S["arr%d" % c], landed)
+        P.matmul_mx(ybank[c], T.w2q[:, CW:2 * CW], T.w2s[:, CW:2 * CW],
+                    T.rq[:, CW * c:CW * c + CW], T.rs[:, CW * c:CW * c + CW], False, True).then_inc(S["y%d" % c], 1)
+
+    _, dst, via_q, via_s = _route(T, topo, rank)
+    to_q = dst if via_q == core else via_q
+    to_s = dst if via_s == core else via_s
+    left = 0
+    for c in range(NCH):
+        g.wait_ge(S["qh%d" % c], 1)
+        left += _send(g, T, topo, core, to_q, _codes(T.rq, c), _codes(T.hq, c), S["arr%d" % c])
+        left += _send(g, T, topo, core, to_s, _plane(T.rs, c), _plane(T.hs, c), S["arr%d" % c])
+    g.wait_ge(S.sent, left)
+
+    Y.wait_ge(S.mu0, G)
+    Y.wait_ge(S.mu1, G)
+    Y.wait_ge(S.sent, left)
+    Y.dma_start(T.h[:], T.ht[:]).then_inc(S.sh, 16)
+    for c in range(NCH):
+        Y.wait_ge(S["yc%d" % c], 1)
+        Y.dma_start(T.y[:, CW * c:CW * c + CW], T.yt[:, CW * c:CW * c + CW]).then_inc(S["sy%d" % c], 16)
+    Y.wait_ge(S.sh, 16)
+    for c in range(NCH):
+        Y.wait_ge(S["sy%d" % c], 16)

@@ -1,4 +1,4 @@
-from concourse.mybir import dt, AluOpType, ActivationFunctionType
+from concourse.mybir import dt, AluOpType, AxisListType, ActivationFunctionType
 
 NCH = 2
 CW = 128
@@ -17,22 +17,25 @@ SCRATCH = {
     "hq": ("sbuf", [128, 256], "float8_e4m3fn_x4"), "hs": ("sbuf", [128, 256], "uint8"),
     "rq": ("sbuf", [128, 256], "float8_e4m3fn_x4"), "rs": ("sbuf", [128, 256], "uint8"),
     "sq": ("sbuf", [128, 1024], "float32"),
-    "zs": ("sbuf", [128, 1024], "float32"),
+    "zc": ("sbuf", [128, 512], "float32"),
+    "rb": ("sbuf", [128, 1024], "bfloat16"),
     "ones": ("sbuf", [128, 128], "float32"),
     "ident": ("sbuf", [128, 128], "float32"),
-    "cinv": ("sbuf", [128, 4], "float32"),
-    "ceps": ("sbuf", [128, 4], "float32"),
-    "rcol": ("sbuf", [128, 8], "float32"),
-    "dg": ("sbuf", [128, 256], "float32"),
+    "identb": ("sbuf", [128, 128], "bfloat16"),
+    "acc": ("sbuf", [128, 4], "float32"),
+    "ss": ("sbuf", [128, 8], "float32"),
+    "rt": ("sbuf", [128, 8], "float32"),
+    "sc": ("sbuf", [128, 8], "float32"),
     "yt": ("sbuf", [128, 256], "float32"),
     "ps": ("psum", [128, 4096], "float32"),
 }
 
 SEMAPHORES = (
-    ["lx0", "lx1", "lw2", "on", "cs", "idn", "qx0", "qx1", "qw2", "sent", "sh"]
+    ["lx0", "lx1", "lw2", "on", "idn", "idb", "qx0", "qx1", "qw2", "sent", "sh", "sq0", "mx1", "cp1", "sq1", "sv1", "sa1"]
     + ["lw1_%d" % b for b in range(G)] + ["qw1_%d" % b for b in range(G)]
-    + ["%s%d%d" % (n, c, b) for n in ("mx", "sq", "cp") for c in range(NCH) for b in range(G)]
-    + ["%s%d" % (n, c) for n in ("st", "r", "d", "bc", "mu", "qh", "arr", "y", "yc", "sy") for c in range(NCH)]
+    + ["mx0%d" % b for b in range(G)] + ["sc0%d" % b for b in range(G)]
+    + ["tr%d%d" % (c, b) for c in range(NCH) for b in range(G)]
+    + ["%s%d" % (n, c) for n in ("st", "rt", "r", "mu", "qh", "arr", "y", "yc", "sy") for c in range(NCH)]
 )
 
 
@@ -91,21 +94,25 @@ def rank_program(g, core, T, topo):
     S = T.sem
     n = len(T.cores)
     V, A, P, Y = g.vector, g.scalar, g.tensor, g.sync
-    mult = AluOpType.mult
+    mult, add = AluOpType.mult, AluOpType.add
     Act = ActivationFunctionType
 
-    def bank(k, a=0, b=CW):
-        return T.ps[:, 512 * k + a:512 * k + b]
-
     def z(c, b):
-        return bank(G * c + b)
+        k = G * c + b
+        return T.ps[:, 512 * k:512 * k + CW]
+
+    z1 = T.ps[:, 512 * G:512 * G + 512]
 
     def piece(buf, c, b):
         return buf[:, 512 * c + CW * b:512 * c + CW * b + CW]
 
-    stat = [bank(7, 128, 129), bank(3, 128, 129)]
-    spread = [bank(0), bank(4)]
-    ybank = [bank(1), bank(2)]
+    def col(buf, c):
+        return buf[:, 4 * c:4 * c + 1]
+
+    def lane(c, b):
+        return T.ht[:, 512 * c + b:512 * c + 512:4]
+
+    ybank = [z(0, 0), z(0, 1)]
 
     Y.dma_start(T.xt[:, 0:512], T.x[:, 0:512]).then_inc(S.lx0, 16)
     A.dma_start(T.w1t[:, 0:512], T.w1[:, 0:512]).then_inc(S.lw1_0, 16)
@@ -117,10 +124,31 @@ def rank_program(g, core, T, topo):
     Y.dma_start(T.w2t[:], T.w2[:]).then_inc(S.lw2, 16)
 
     V.memset(T.ones[:], 1.0).then_inc(S.on, 1)
-    V.memset(T.cinv[:], 1.0 / ROWS).then_inc(S.cs, 1)
-    V.memset(T.ceps[:], EPS / 128.0).then_inc(S.cs, 1)
     g.wait_ge(S.on, 1)
     g.affine_select(T.ident[:], T.ones[:], [[-1, 128]], AluOpType.is_equal, 0.0, 0, 1).then_inc(S.idn, 1)
+    V.wait_ge(S.idn, 1)
+    V.tensor_copy(T.identb[:], T.ident[:]).then_inc(S.idb, 1)
+
+    def scale0(q, b):
+        q.wait_ge(S["mx0%d" % b], 1)
+        if q is V:
+            i = V.tensor_scalar(piece(T.rb, 0, b), z(0, b), col(T.sc, 0), None, mult)
+        else:
+            i = A.activation(piece(T.rb, 0, b), z(0, b), Act.Copy, scale=col(T.sc, 0))
+        i.then_inc(S["sc0%d" % b], 1)
+
+    def into_tile(q, c, b):
+        q.wait_ge(S["tr%d%d" % (c, b)], 1)
+        if q is V:
+            i = V.tensor_copy(lane(c, b), z(c, b))
+        else:
+            i = A.activation(lane(c, b), z(c, b), Act.Copy)
+        i.then_inc(S["mu%d" % c], 1)
+
+    def quantise_h(c):
+        V.wait_ge(S["mu%d" % c], G)
+        V.quantize_mx(T.hq[:, CW * c:CW * c + CW], T.hs[:, CW * c:CW * c + CW],
+                      T.ht[:, 512 * c:512 * c + 512]).then_inc(S["qh%d" % c], 1)
 
     V.wait_ge(S.lx0, 16)
     V.quantize_mx(T.xq[:, 0:CW], T.xs[:, 0:CW], T.xt[:, 0:512]).then_inc(S.qx0, 1)
@@ -128,26 +156,31 @@ def rank_program(g, core, T, topo):
         V.wait_ge(S["lw1_%d" % b], 16)
         V.quantize_mx(T.w1q[:, CW * b:CW * b + CW], T.w1s[:, CW * b:CW * b + CW],
                       T.w1t[:, 512 * b:512 * b + 512]).then_inc(S["qw1_%d" % b], 1)
-    V.wait_ge(S.st0, 1)
-    V.reciprocal(T.rcol[:, 0:1], stat[0]).then_inc(S.r0, 1)
     V.wait_ge(S.lx1, 16)
     V.quantize_mx(T.xq[:, CW:2 * CW], T.xs[:, CW:2 * CW], T.xt[:, 512:1024]).then_inc(S.qx1, 1)
-    for b in range(G):
-        V.wait_ge(S["mx1%d" % b], 1)
-        V.tensor_copy(piece(T.zs, 1, b), z(1, b)).then_inc(S["cp1%d" % b], 1)
-        V.wait_ge(S["cp1%d" % b], 1)
-        V.tensor_tensor(piece(T.sq, 1, b), z(1, b), piece(T.zs, 1, b), mult).then_inc(S["sq1%d" % b], 1)
-    V.wait_ge(S.st1, 1)
-    V.reciprocal(T.rcol[:, 4:5], stat[1]).then_inc(S.r1, 1)
-    for c in range(NCH):
-        V.wait_ge(S["bc%d" % c], 1)
-        for b in range(G):
-            V.wait_ge(S["cp%d%d" % (c, b)], 1)
-            V.tensor_tensor(T.ht[:, 512 * c + b:512 * c + 512:4], piece(T.zs, c, b), spread[c], mult
-                            ).then_inc(S["mu%d" % c], 1)
-        V.wait_ge(S["mu%d" % c], G)
-        V.quantize_mx(T.hq[:, CW * c:CW * c + CW], T.hs[:, CW * c:CW * c + CW],
-                      T.ht[:, 512 * c:512 * c + 512]).then_inc(S["qh%d" % c], 1)
+    V.wait_ge(S.sq0, G)
+    V.tensor_reduce(col(T.ss, 0), T.acc[:, 0:G], AxisListType.X, add).then_inc(S.st0, 1)
+    V.wait_ge(S.mx1, 1)
+    V.tensor_copy(T.zc[:], z1).then_inc(S.cp1, 1)
+    V.wait_ge(S.cp1, 1)
+    V.tensor_tensor(T.sq[:, 512:1024], z1, T.zc[:], mult).then_inc(S.sq1, 1)
+    V.wait_ge(S.rt0, 1)
+    V.reciprocal(col(T.sc, 0), col(T.rt, 0)).then_inc(S.r0, 1)
+    V.wait_ge(S.r0, 1)
+    scale0(V, 0)
+    scale0(V, 2)
+    V.wait_ge(S.sq1, 1)
+    V.tensor_reduce(col(T.ss, 1), T.sq[:, 512:1024], AxisListType.X, add).then_inc(S.st1, 1)
+    into_tile(V, 0, 0)
+    into_tile(V, 0, 2)
+    quantise_h(0)
+    V.wait_ge(S.rt1, 1)
+    V.reciprocal(col(T.sc, 1), col(T.rt, 1)).then_inc(S.r1, 1)
+    V.wait_ge(S.r1, 1)
+    V.tensor_scalar(T.rb[:, 512:768], T.zc[:, 0:256], col(T.sc, 1), None, mult).then_inc(S.sv1, 1)
+    into_tile(V, 1, 0)
+    into_tile(V, 1, 1)
+    quantise_h(1)
     V.wait_ge(S.lw2, 16)
     V.quantize_mx(T.w2q[:], T.w2s[:], T.w2t[:]).then_inc(S.qw2, 1)
     for c in range(NCH):
@@ -156,58 +189,48 @@ def rank_program(g, core, T, topo):
 
     for b in range(G):
         A.wait_ge(S["mx0%d" % b], 1)
-        A.activation(piece(T.sq, 0, b), z(0, b), Act.Square).then_inc(S["sq0%d" % b], 1)
-    for b in range(G):
-        A.activation(piece(T.zs, 0, b), z(0, b), Act.Copy).then_inc(S["cp0%d" % b], 1)
-    A.wait_ge(S.idn, 1)
-    for c in range(NCH):
-        A.wait_ge(S["r%d" % c], 1)
-        A.activation(T.dg[:, CW * c:CW * c + CW], T.ident[:], Act.Sqrt,
-                     scale=T.rcol[:, 4 * c:4 * c + 1]).then_inc(S["d%d" % c], 1)
+        A.activation(piece(T.sq, 0, b), z(0, b), Act.Square, accum_out=T.acc[:, b:b + 1]).then_inc(S.sq0, 1)
+    A.wait_ge(S.st0, 1)
+    A.activation(col(T.rt, 0), col(T.ss, 0), Act.Sqrt, bias=EPS, scale=1.0 / ROWS).then_inc(S.rt0, 1)
+    A.wait_ge(S.r0, 1)
+    scale0(A, 1)
+    scale0(A, 3)
+    into_tile(A, 0, 1)
+    into_tile(A, 0, 3)
+    A.wait_ge(S.st1, 1)
+    A.activation(col(T.rt, 1), col(T.ss, 1), Act.Sqrt, bias=EPS, scale=1.0 / ROWS).then_inc(S.rt1, 1)
+    A.wait_ge(S.r1, 1)
+    A.wait_ge(S.cp1, 1)
+    A.activation(T.rb[:, 768:1024], T.zc[:, 256:512], Act.Copy, scale=col(T.sc, 1)).then_inc(S.sa1, 1)
+    into_tile(A, 1, 2)
+    into_tile(A, 1, 3)
 
-    def layer1(c, b):
-        P.matmul_mx(z(c, b), T.w1q[:, CW * b:CW * b + CW], T.w1s[:, CW * b:CW * b + CW],
-                    T.xq[:, CW * c:CW * c + CW], T.xs[:, CW * c:CW * c + CW], True, True).then_inc(S["mx%d%d" % (c, b)], 1)
-
-    def mean(c, b):
-        P.wait_ge(S["sq%d%d" % (c, b)], 1)
-        i = P.matmul(stat[c], piece(T.sq, c, b), T.cinv[:, 0:1], False, b == G - 1)
-        if b == G - 1:
-            i.then_inc(S["st%d" % c], 1)
-
-    P.wait_ge(S.on, 1)
-    P.wait_ge(S.cs, 2)
-    P.matmul(stat[0], T.ones[:], T.ceps[:, 0:1], True, False)
     P.wait_ge(S.qx0, 1)
-    P.wait_ge(S.qw1_0, 1)
-    layer1(0, 0)
-    P.wait_ge(S.qw1_1, 1)
-    layer1(0, 1)
-    mean(0, 0)
-    P.wait_ge(S.qw1_2, 1)
-    layer1(0, 2)
-    mean(0, 1)
-    P.wait_ge(S.qw1_3, 1)
-    layer1(0, 3)
-    mean(0, 2)
-    mean(0, 3)
-    P.wait_ge(S.qx1, 1)
-    layer1(1, 0)
-    layer1(1, 1)
-    layer1(1, 2)
-    P.wait_ge(S.r0, 1)
-    layer1(1, 3)
-    P.wait_ge(S.cp03, 1)
-    P.matmul(stat[1], T.ones[:], T.ceps[:, 0:1], True, False)
     for b in range(G):
-        mean(1, b)
-    P.wait_ge(S.cp00, 1)
-    for c in range(NCH):
-        P.wait_ge(S["d%d" % c], 1)
-        P.matmul(spread[c], T.ones[:], T.dg[:, CW * c:CW * c + CW], True, True).then_inc(S["bc%d" % c], 1)
+        P.wait_ge(S["qw1_%d" % b], 1)
+        P.matmul_mx(z(0, b), T.xq[:, 0:CW], T.xs[:, 0:CW],
+                    T.w1q[:, CW * b:CW * b + CW], T.w1s[:, CW * b:CW * b + CW], True, True).then_inc(S["mx0%d" % b], 1)
+    P.wait_ge(S.qx1, 1)
+    P.matmul_mx(z1, T.xq[:, CW:2 * CW], T.xs[:, CW:2 * CW], T.w1q[:], T.w1s[:], True, True).then_inc(S.mx1, 1)
+    P.wait_ge(S.idb, 1)
+    P.wait_ge(S.sq0, G)
+
+    def turn(c, b):
+        P.matmul(z(c, b), piece(T.rb, c, b), T.identb[:], True, True).then_inc(S["tr%d%d" % (c, b)], 1)
+
+    for b in range(G):
+        P.wait_ge(S["sc0%d" % b], 1)
+        turn(0, b)
+    P.wait_ge(S.cp1, 1)
+    P.wait_ge(S.sq1, 1)
+    P.wait_ge(S.sv1, 1)
+    turn(1, 0)
+    P.wait_ge(S.sa1, 1)
+    turn(1, 2)
+    turn(1, 1)
+    turn(1, 3)
     P.wait_ge(S.qw2, 1)
-    P.wait_ge(S.cp01, 1)
-    P.wait_ge(S.cp02, 1)
+    P.wait_ge(S.mu0, G)
     for c in range(NCH):
         P.wait_ge(S["qh%d" % c], 1)
         P.matmul_mx(ybank[c], T.w2q[:, 0:CW], T.w2s[:, 0:CW],

@@ -5,6 +5,7 @@ CW = 128
 G = 4
 EPS = 0.001
 ROWS = 512
+RS = ROWS ** -0.5
 
 SCRATCH = {
     "xt": ("sbuf", [128, 1024], "bfloat16"),
@@ -17,13 +18,13 @@ SCRATCH = {
     "hq": ("sbuf", [128, 256], "float8_e4m3fn_x4"), "hs": ("sbuf", [128, 256], "uint8"),
     "rq": ("sbuf", [128, 256], "float8_e4m3fn_x4"), "rs": ("sbuf", [128, 256], "uint8"),
     "sq": ("sbuf", [128, 1024], "float32"),
-    "zc": ("sbuf", [128, 512], "float32"),
     "rb": ("sbuf", [128, 1024], "bfloat16"),
     "ones": ("sbuf", [128, 128], "float32"),
     "ident": ("sbuf", [128, 128], "float32"),
     "identb": ("sbuf", [128, 128], "bfloat16"),
-    "acc": ("sbuf", [128, 4], "float32"),
-    "ss": ("sbuf", [128, 8], "float32"),
+    "acc": ("sbuf", [128, 8], "float32"),
+    "bi": ("sbuf", [128, 8], "float32"),
+    "a1": ("sbuf", [128, 8], "float32"),
     "rt": ("sbuf", [128, 8], "float32"),
     "sc": ("sbuf", [128, 8], "float32"),
     "yt": ("sbuf", [128, 256], "float32"),
@@ -31,11 +32,12 @@ SCRATCH = {
 }
 
 SEMAPHORES = (
-    ["lx0", "lx1", "lw2", "on", "idn", "idb", "qx0", "qx1", "qw2", "sent", "sh", "sq0", "mx1", "cp1", "sq1", "sv1", "sa1"]
+    ["lx0", "lx1", "lw2", "on", "ep", "idn", "idb", "qx0", "qx1", "qw2", "sent", "sh", "bi0", "q0", "rq0",
+     "mx1a", "mx1b", "s1a", "s1b", "s1e"]
     + ["lw1_%d" % b for b in range(G)] + ["qw1_%d" % b for b in range(G)]
-    + ["mx0%d" % b for b in range(G)] + ["sc0%d" % b for b in range(G)]
-    + ["tr%d%d" % (c, b) for c in range(NCH) for b in range(G)]
-    + ["%s%d" % (n, c) for n in ("st", "rt", "r", "mu", "qh", "arr", "y", "yc", "sy") for c in range(NCH)]
+    + ["mx0%d" % b for b in range(G)] + ["sqd%d" % b for b in range(G)]
+    + ["%s%d%d" % (k, c, b) for k in ("sc", "tr") for c in range(NCH) for b in range(G)]
+    + ["%s%d" % (k, c) for k in ("rt", "r", "mu", "qh", "arr", "y", "yc", "sy") for c in range(NCH)]
 )
 
 
@@ -52,6 +54,10 @@ def _route(T, topo, s):
                if topo.chip(k) == topo.chip(src) and topo.die(k) == topo.die(src)
                and T.rank_of(k) is None and topo.may_write(k, dst)]
     return src, dst, helpers[0], helpers[1]
+
+
+def _via(route, c):
+    return (route[2], route[3]) if c % 2 == 0 else (route[3], route[2])
 
 
 def _send(g, T, topo, src, dst, out_ap, in_ap, sem):
@@ -72,14 +78,15 @@ def _plane(buf, c):
 
 def _helper_program(g, core, T, topo):
     for s in range(len(T.cores)):
-        src, dst, via_q, via_s = _route(T, topo, s)
-        if core == src or core not in (via_q, via_s):
+        route = _route(T, topo, s)
+        src, dst = route[0], route[1]
+        if core == src or core not in (route[2], route[3]):
             continue
         got = _engines(topo.mask(src, core))
         left = 0
         for c in range(NCH):
             g.wait_ge(T.sem["arr%d" % c], got)
-            if core == via_q:
+            if core == _via(route, c)[0]:
                 left += _send(g, T, topo, core, dst, _codes(T.rq, c), _codes(T.rq, c), T.sem["arr%d" % c])
             else:
                 left += _send(g, T, topo, core, dst, _plane(T.rs, c), _plane(T.rs, c), T.sem["arr%d" % c])
@@ -97,11 +104,16 @@ def rank_program(g, core, T, topo):
     mult, add = AluOpType.mult, AluOpType.add
     Act = ActivationFunctionType
 
-    def z(c, b):
-        k = G * c + b
-        return T.ps[:, 512 * k:512 * k + CW]
+    def bank(k, w=CW, a=0):
+        return T.ps[:, 512 * k + a:512 * k + a + w]
 
-    z1 = T.ps[:, 512 * G:512 * G + 512]
+    def z(c, b):
+        return bank(b) if c == 0 else bank((6, 7, 2, 3)[b])
+
+    zA, zB = bank(4, 256), bank(5, 256)
+
+    def raw1(b):
+        return bank(4 + b // 2, CW, CW * (b % 2))
 
     def piece(buf, c, b):
         return buf[:, 512 * c + CW * b:512 * c + CW * b + CW]
@@ -112,7 +124,12 @@ def rank_program(g, core, T, topo):
     def lane(c, b):
         return T.ht[:, 512 * c + b:512 * c + 512:4]
 
-    ybank = [z(0, 0), z(0, 1)]
+    def share(b):
+        k = b if b < G - 1 else G
+        return T.acc[:, k:k + 1]
+
+    rq0 = T.bi[:, 2:3]
+    ybank = [bank(0), bank(1)]
 
     Y.dma_start(T.xt[:, 0:512], T.x[:, 0:512]).then_inc(S.lx0, 16)
     A.dma_start(T.w1t[:, 0:512], T.w1[:, 0:512]).then_inc(S.lw1_0, 16)
@@ -124,18 +141,21 @@ def rank_program(g, core, T, topo):
     Y.dma_start(T.w2t[:], T.w2[:]).then_inc(S.lw2, 16)
 
     V.memset(T.ones[:], 1.0).then_inc(S.on, 1)
+    V.memset(T.acc[:, G - 1:G], EPS).then_inc(S.ep, 1)
     g.wait_ge(S.on, 1)
     g.affine_select(T.ident[:], T.ones[:], [[-1, 128]], AluOpType.is_equal, 0.0, 0, 1).then_inc(S.idn, 1)
     V.wait_ge(S.idn, 1)
     V.tensor_copy(T.identb[:], T.ident[:]).then_inc(S.idb, 1)
 
-    def scale0(q, b):
-        q.wait_ge(S["mx0%d" % b], 1)
-        if q is V:
-            i = V.tensor_scalar(piece(T.rb, 0, b), z(0, b), col(T.sc, 0), None, mult)
+    def scale(q, c, b):
+        src = z(0, b) if c == 0 else raw1(b)
+        if q is A:
+            i = A.activation(piece(T.rb, c, b), src, Act.Copy, scale=col(T.sc, c))
+        elif c == 0:
+            i = V.tensor_scalar(piece(T.rb, c, b), src, col(T.rt, 0), rq0, mult, mult)
         else:
-            i = A.activation(piece(T.rb, 0, b), z(0, b), Act.Copy, scale=col(T.sc, 0))
-        i.then_inc(S["sc0%d" % b], 1)
+            i = V.tensor_scalar(piece(T.rb, c, b), src, col(T.sc, c), None, mult)
+        i.then_inc(S["sc%d%d" % (c, b)], 1)
 
     def into_tile(q, c, b):
         q.wait_ge(S["tr%d%d" % (c, b)], 1)
@@ -156,28 +176,29 @@ def rank_program(g, core, T, topo):
         V.wait_ge(S["lw1_%d" % b], 16)
         V.quantize_mx(T.w1q[:, CW * b:CW * b + CW], T.w1s[:, CW * b:CW * b + CW],
                       T.w1t[:, 512 * b:512 * b + 512]).then_inc(S["qw1_%d" % b], 1)
+    V.wait_ge(S.ep, 1)
+    for b in range(G - 1):
+        V.wait_ge(S["sqd%d" % b], 1)
+    V.tensor_reduce(T.bi[:, 0:1], T.acc[:, 0:G], AxisListType.X, add).then_inc(S.bi0, 1)
     V.wait_ge(S.lx1, 16)
     V.quantize_mx(T.xq[:, CW:2 * CW], T.xs[:, CW:2 * CW], T.xt[:, 512:1024]).then_inc(S.qx1, 1)
-    V.wait_ge(S.sq0, G)
-    V.tensor_reduce(col(T.ss, 0), T.acc[:, 0:G], AxisListType.X, add).then_inc(S.st0, 1)
-    V.wait_ge(S.mx1, 1)
-    V.tensor_copy(T.zc[:], z1).then_inc(S.cp1, 1)
-    V.wait_ge(S.cp1, 1)
-    V.tensor_tensor(T.sq[:, 512:1024], z1, T.zc[:], mult).then_inc(S.sq1, 1)
+    V.wait_ge(S["sqd%d" % (G - 1)], 1)
+    V.tensor_reduce(T.bi[:, 1:2], T.acc[:, 0:G + 1], AxisListType.X, add).then_inc(S.q0, 1)
+    V.wait_ge(S.q0, 1)
+    V.reciprocal(rq0, T.bi[:, 1:2]).then_inc(S.rq0, 1)
+    V.wait_ge(S.rq0, 1)
     V.wait_ge(S.rt0, 1)
-    V.reciprocal(col(T.sc, 0), col(T.rt, 0)).then_inc(S.r0, 1)
-    V.wait_ge(S.r0, 1)
-    scale0(V, 0)
-    scale0(V, 2)
-    V.wait_ge(S.sq1, 1)
-    V.tensor_reduce(col(T.ss, 1), T.sq[:, 512:1024], AxisListType.X, add).then_inc(S.st1, 1)
-    into_tile(V, 0, 0)
-    into_tile(V, 0, 2)
+    scale(V, 0, 0)
+    scale(V, 0, 2)
+    for b in range(G):
+        into_tile(V, 0, b)
     quantise_h(0)
     V.wait_ge(S.rt1, 1)
     V.reciprocal(col(T.sc, 1), col(T.rt, 1)).then_inc(S.r1, 1)
     V.wait_ge(S.r1, 1)
-    V.tensor_scalar(T.rb[:, 512:768], T.zc[:, 0:256], col(T.sc, 1), None, mult).then_inc(S.sv1, 1)
+    V.wait_ge(S.mx1a, 1)
+    scale(V, 1, 0)
+    scale(V, 1, 1)
     into_tile(V, 1, 0)
     into_tile(V, 1, 1)
     quantise_h(1)
@@ -189,19 +210,28 @@ def rank_program(g, core, T, topo):
 
     for b in range(G):
         A.wait_ge(S["mx0%d" % b], 1)
-        A.activation(piece(T.sq, 0, b), z(0, b), Act.Square, accum_out=T.acc[:, b:b + 1]).then_inc(S.sq0, 1)
-    A.wait_ge(S.st0, 1)
-    A.activation(col(T.rt, 0), col(T.ss, 0), Act.Sqrt, bias=EPS, scale=1.0 / ROWS).then_inc(S.rt0, 1)
+        A.activation(piece(T.sq, 0, b), z(0, b), Act.Square, scale=RS, accum_out=share(b)).then_inc(S["sqd%d" % b], 1)
+    A.wait_ge(S.bi0, 1)
+    A.wait_ge(S["sqd%d" % (G - 1)], 1)
+    A.activation(col(T.rt, 0), share(G - 1), Act.Sqrt, bias=T.bi[:, 0:1]).then_inc(S.rt0, 1)
+    A.wait_ge(S.rq0, 1)
+    A.wait_ge(S.rt0, 1)
+    A.activation(col(T.sc, 0), col(T.rt, 0), Act.Copy, scale=rq0).then_inc(S.r0, 1)
     A.wait_ge(S.r0, 1)
-    scale0(A, 1)
-    scale0(A, 3)
-    into_tile(A, 0, 1)
-    into_tile(A, 0, 3)
-    A.wait_ge(S.st1, 1)
-    A.activation(col(T.rt, 1), col(T.ss, 1), Act.Sqrt, bias=EPS, scale=1.0 / ROWS).then_inc(S.rt1, 1)
+    scale(A, 0, 1)
+    scale(A, 0, 3)
+    A.wait_ge(S.mx1a, 1)
+    A.activation(T.sq[:, 512:768], zA, Act.Square, scale=RS, accum_out=T.a1[:, 0:1]).then_inc(S.s1a, 1)
+    A.wait_ge(S.mx1b, 1)
+    A.activation(T.sq[:, 768:1024], zB, Act.Square, scale=RS, accum_out=T.a1[:, 2:3]).then_inc(S.s1b, 1)
+    A.wait_ge(S.s1a, 1)
+    A.activation(T.a1[:, 1:2], T.a1[:, 0:1], Act.Identity, bias=EPS).then_inc(S.s1e, 1)
+    A.wait_ge(S.s1b, 1)
+    A.wait_ge(S.s1e, 1)
+    A.activation(col(T.rt, 1), T.a1[:, 2:3], Act.Sqrt, bias=T.a1[:, 1:2]).then_inc(S.rt1, 1)
     A.wait_ge(S.r1, 1)
-    A.wait_ge(S.cp1, 1)
-    A.activation(T.rb[:, 768:1024], T.zc[:, 256:512], Act.Copy, scale=col(T.sc, 1)).then_inc(S.sa1, 1)
+    scale(A, 1, 2)
+    scale(A, 1, 3)
     into_tile(A, 1, 2)
     into_tile(A, 1, 3)
 
@@ -211,42 +241,38 @@ def rank_program(g, core, T, topo):
         P.matmul_mx(z(0, b), T.xq[:, 0:CW], T.xs[:, 0:CW],
                     T.w1q[:, CW * b:CW * b + CW], T.w1s[:, CW * b:CW * b + CW], True, True).then_inc(S["mx0%d" % b], 1)
     P.wait_ge(S.qx1, 1)
-    P.matmul_mx(z1, T.xq[:, CW:2 * CW], T.xs[:, CW:2 * CW], T.w1q[:], T.w1s[:], True, True).then_inc(S.mx1, 1)
+    P.matmul_mx(zA, T.xq[:, CW:2 * CW], T.xs[:, CW:2 * CW], T.w1q[:, 0:256], T.w1s[:, 0:256], True, True).then_inc(S.mx1a, 1)
+    P.matmul_mx(zB, T.xq[:, CW:2 * CW], T.xs[:, CW:2 * CW], T.w1q[:, 256:512], T.w1s[:, 256:512], True, True).then_inc(S.mx1b, 1)
     P.wait_ge(S.idb, 1)
-    P.wait_ge(S.sq0, G)
 
     def turn(c, b):
+        P.wait_ge(S["sc%d%d" % (c, b)], 1)
         P.matmul(z(c, b), piece(T.rb, c, b), T.identb[:], True, True).then_inc(S["tr%d%d" % (c, b)], 1)
 
     for b in range(G):
-        P.wait_ge(S["sc0%d" % b], 1)
+        P.wait_ge(S["sqd%d" % b], 1)
         turn(0, b)
-    P.wait_ge(S.cp1, 1)
-    P.wait_ge(S.sq1, 1)
-    P.wait_ge(S.sv1, 1)
-    turn(1, 0)
-    P.wait_ge(S.sa1, 1)
-    turn(1, 2)
-    turn(1, 1)
-    turn(1, 3)
-    P.wait_ge(S.qw2, 1)
     P.wait_ge(S.mu0, G)
+    for b in (0, 2, 1, 3):
+        turn(1, b)
+    P.wait_ge(S.qw2, 1)
     for c in range(NCH):
         P.wait_ge(S["qh%d" % c], 1)
         P.matmul_mx(ybank[c], T.w2q[:, 0:CW], T.w2s[:, 0:CW],
                     T.hq[:, CW * c:CW * c + CW], T.hs[:, CW * c:CW * c + CW], True, False)
-    _, _, in_q, in_s = _route(T, topo, (rank + 1) % n)
-    landed = _engines(topo.mask(in_q, core)) + _engines(topo.mask(in_s, core))
+    inc = _route(T, topo, (rank + 1) % n)
+    landed = _engines(topo.mask(inc[2], core)) + _engines(topo.mask(inc[3], core))
     for c in range(NCH):
         P.wait_ge(S["arr%d" % c], landed)
         P.matmul_mx(ybank[c], T.w2q[:, CW:2 * CW], T.w2s[:, CW:2 * CW],
                     T.rq[:, CW * c:CW * c + CW], T.rs[:, CW * c:CW * c + CW], False, True).then_inc(S["y%d" % c], 1)
 
-    _, dst, via_q, via_s = _route(T, topo, rank)
-    to_q = dst if via_q == core else via_q
-    to_s = dst if via_s == core else via_s
+    out = _route(T, topo, rank)
     left = 0
     for c in range(NCH):
+        via_q, via_s = _via(out, c)
+        to_q = out[1] if via_q == core else via_q
+        to_s = out[1] if via_s == core else via_s
         g.wait_ge(S["qh%d" % c], 1)
         left += _send(g, T, topo, core, to_q, _codes(T.rq, c), _codes(T.hq, c), S["arr%d" % c])
         left += _send(g, T, topo, core, to_s, _plane(T.rs, c), _plane(T.hs, c), S["arr%d" % c])

from concourse.mybir import dt, AluOpType, AxisListType, ActivationFunctionType

NCH = 2
CW = 128
G = 4
EPS = 0.001
ROWS = 512
RS = ROWS ** -0.5

SCRATCH = {
    "xt": ("sbuf", [128, 1024], "bfloat16"),
    "w1t": ("sbuf", [128, 2048], "bfloat16"),
    "w2t": ("sbuf", [128, 1024], "bfloat16"),
    "xq": ("sbuf", [128, 256], "float8_e4m3fn_x4"), "xs": ("sbuf", [128, 256], "uint8"),
    "w1q": ("sbuf", [128, 512], "float8_e4m3fn_x4"), "w1s": ("sbuf", [128, 512], "uint8"),
    "w2q": ("sbuf", [128, 256], "float8_e4m3fn_x4"), "w2s": ("sbuf", [128, 256], "uint8"),
    "ht": ("sbuf", [128, 1024], "bfloat16"),
    "hq": ("sbuf", [128, 256], "float8_e4m3fn_x4"), "hs": ("sbuf", [128, 256], "uint8"),
    "rq": ("sbuf", [128, 256], "float8_e4m3fn_x4"), "rs": ("sbuf", [128, 256], "uint8"),
    "sq": ("sbuf", [128, 1024], "float32"),
    "rb": ("sbuf", [128, 1024], "bfloat16"),
    "ones": ("sbuf", [128, 128], "float32"),
    "ident": ("sbuf", [128, 128], "float32"),
    "identb": ("sbuf", [128, 128], "bfloat16"),
    "acc": ("sbuf", [128, 8], "float32"),
    "bi": ("sbuf", [128, 8], "float32"),
    "a1": ("sbuf", [128, 8], "float32"),
    "rt": ("sbuf", [128, 8], "float32"),
    "sc": ("sbuf", [128, 8], "float32"),
    "yt": ("sbuf", [128, 256], "float32"),
    "ps": ("psum", [128, 4096], "float32"),
}

SEMAPHORES = (
    ["lx0", "lx1", "lw2", "on", "ep", "idn", "idb", "qx0", "qx1", "qw2", "sent", "sh", "bi0", "q0", "rq0",
     "mx1a", "mx1b", "s1a", "s1b", "s1e"]
    + ["lw1_%d" % b for b in range(G)] + ["qw1_%d" % b for b in range(G)]
    + ["mx0%d" % b for b in range(G)] + ["sqd%d" % b for b in range(G)]
    + ["%s%d%d" % (k, c, b) for k in ("sc", "tr") for c in range(NCH) for b in range(G)]
    + ["%s%d" % (k, c) for k in ("rt", "r", "mu", "qh", "arr", "y", "yc", "sy") for c in range(NCH)]
)


def _engines(mask):
    return bin(mask).count("1")


def _route(T, topo, s):
    n = len(T.cores)
    src, dst = T.cores[s], T.cores[(s - 1) % n]
    if topo.may_write(src, dst):
        return src, dst, src, src
    helpers = [k for k in range(topo.CORES_PER_CHIP * topo.CHIPS)
               if topo.chip(k) == topo.chip(src) and topo.die(k) == topo.die(src)
               and T.rank_of(k) is None and topo.may_write(k, dst)]
    return src, dst, helpers[0], helpers[1]


def _via(route, c):
    return (route[2], route[3]) if c % 2 == 0 else (route[3], route[2])


def _send(g, T, topo, src, dst, out_ap, in_ap, sem):
    rid, pid, _ = topo.addr(dst)
    m = topo.mask(src, dst)
    g.remote_dma(out_ap=out_ap, in_ap=in_ap, remote_sem=sem, local_sem=T.sem.sent,
                 pid=pid, routing_id=rid, dma_engine_mask=m)
    return _engines(m)


def _codes(buf, c):
    return buf[:, CW * c:CW * c + CW].bitcast(dt.uint8)


def _plane(buf, c):
    return buf[:, CW * c:CW * c + CW]


def _helper_program(g, core, T, topo):
    for s in range(len(T.cores)):
        route = _route(T, topo, s)
        src, dst = route[0], route[1]
        if core == src or core not in (route[2], route[3]):
            continue
        got = _engines(topo.mask(src, core))
        left = 0
        for c in range(NCH):
            g.wait_ge(T.sem["arr%d" % c], got)
            if core == _via(route, c)[0]:
                left += _send(g, T, topo, core, dst, _codes(T.rq, c), _codes(T.rq, c), T.sem["arr%d" % c])
            else:
                left += _send(g, T, topo, core, dst, _plane(T.rs, c), _plane(T.rs, c), T.sem["arr%d" % c])
        g.wait_ge(T.sem.sent, left)


def rank_program(g, core, T, topo):
    rank = T.rank_of(core)
    if rank is None:
        _helper_program(g, core, T, topo)
        return
    S = T.sem
    n = len(T.cores)
    V, A, P, Y = g.vector, g.scalar, g.tensor, g.sync
    mult, add = AluOpType.mult, AluOpType.add
    Act = ActivationFunctionType

    def bank(k, w=CW, a=0):
        return T.ps[:, 512 * k + a:512 * k + a + w]

    def z(c, b):
        return bank(b) if c == 0 else bank((6, 7, 2, 3)[b])

    zA, zB = bank(4, 256), bank(5, 256)

    def raw1(b):
        return bank(4 + b // 2, CW, CW * (b % 2))

    def piece(buf, c, b):
        return buf[:, 512 * c + CW * b:512 * c + CW * b + CW]

    def col(buf, c):
        return buf[:, 4 * c:4 * c + 1]

    def lane(c, b):
        return T.ht[:, 512 * c + b:512 * c + 512:4]

    def share(b):
        k = b if b < G - 1 else G
        return T.acc[:, k:k + 1]

    rq0 = T.bi[:, 2:3]
    ybank = [bank(0), bank(1)]

    Y.dma_start(T.xt[:, 0:512], T.x[:, 0:512]).then_inc(S.lx0, 16)
    A.dma_start(T.w1t[:, 0:512], T.w1[:, 0:512]).then_inc(S.lw1_0, 16)
    Y.dma_start(T.w1t[:, 512:1024], T.w1[:, 512:1024]).then_inc(S.lw1_1, 16)
    A.dma_start(T.w1t[:, 1024:1536], T.w1[:, 1024:1536]).then_inc(S.lw1_2, 16)
    Y.dma_start(T.w1t[:, 1536:2048], T.w1[:, 1536:2048]).then_inc(S.lw1_3, 16)
    Y.dma_start(T.xt[:, 512:1024], T.x[:, 512:1024]).then_inc(S.lx1, 16)
    Y.wait_ge(S.lx0, 16)
    Y.dma_start(T.w2t[:], T.w2[:]).then_inc(S.lw2, 16)

    V.memset(T.ones[:], 1.0).then_inc(S.on, 1)
    V.memset(T.acc[:, G - 1:G], EPS).then_inc(S.ep, 1)
    g.wait_ge(S.on, 1)
    g.affine_select(T.ident[:], T.ones[:], [[-1, 128]], AluOpType.is_equal, 0.0, 0, 1).then_inc(S.idn, 1)
    V.wait_ge(S.idn, 1)
    V.tensor_copy(T.identb[:], T.ident[:]).then_inc(S.idb, 1)

    def scale(q, c, b):
        src = z(0, b) if c == 0 else raw1(b)
        if q is A:
            i = A.activation(piece(T.rb, c, b), src, Act.Copy, scale=col(T.sc, c))
        elif c == 0:
            i = V.tensor_scalar(piece(T.rb, c, b), src, col(T.rt, 0), rq0, mult, mult)
        else:
            i = V.tensor_scalar(piece(T.rb, c, b), src, col(T.sc, c), None, mult)
        i.then_inc(S["sc%d%d" % (c, b)], 1)

    def into_tile(q, c, b):
        q.wait_ge(S["tr%d%d" % (c, b)], 1)
        if q is V:
            i = V.tensor_copy(lane(c, b), z(c, b))
        else:
            i = A.activation(lane(c, b), z(c, b), Act.Copy)
        i.then_inc(S["mu%d" % c], 1)

    def quantise_h(c):
        V.wait_ge(S["mu%d" % c], G)
        V.quantize_mx(T.hq[:, CW * c:CW * c + CW], T.hs[:, CW * c:CW * c + CW],
                      T.ht[:, 512 * c:512 * c + 512]).then_inc(S["qh%d" % c], 1)

    V.wait_ge(S.lx0, 16)
    V.quantize_mx(T.xq[:, 0:CW], T.xs[:, 0:CW], T.xt[:, 0:512]).then_inc(S.qx0, 1)
    for b in range(G):
        V.wait_ge(S["lw1_%d" % b], 16)
        V.quantize_mx(T.w1q[:, CW * b:CW * b + CW], T.w1s[:, CW * b:CW * b + CW],
                      T.w1t[:, 512 * b:512 * b + 512]).then_inc(S["qw1_%d" % b], 1)
    V.wait_ge(S.ep, 1)
    for b in range(G - 1):
        V.wait_ge(S["sqd%d" % b], 1)
    V.tensor_reduce(T.bi[:, 0:1], T.acc[:, 0:G], AxisListType.X, add).then_inc(S.bi0, 1)
    V.wait_ge(S.lx1, 16)
    V.quantize_mx(T.xq[:, CW:2 * CW], T.xs[:, CW:2 * CW], T.xt[:, 512:1024]).then_inc(S.qx1, 1)
    V.wait_ge(S["sqd%d" % (G - 1)], 1)
    V.tensor_reduce(T.bi[:, 1:2], T.acc[:, 0:G + 1], AxisListType.X, add).then_inc(S.q0, 1)
    V.wait_ge(S.q0, 1)
    V.reciprocal(rq0, T.bi[:, 1:2]).then_inc(S.rq0, 1)
    V.wait_ge(S.rq0, 1)
    V.wait_ge(S.rt0, 1)
    scale(V, 0, 0)
    scale(V, 0, 2)
    for b in range(G):
        into_tile(V, 0, b)
    quantise_h(0)
    V.wait_ge(S.rt1, 1)
    V.reciprocal(col(T.sc, 1), col(T.rt, 1)).then_inc(S.r1, 1)
    V.wait_ge(S.r1, 1)
    V.wait_ge(S.mx1a, 1)
    scale(V, 1, 0)
    scale(V, 1, 1)
    into_tile(V, 1, 0)
    into_tile(V, 1, 1)
    quantise_h(1)
    V.wait_ge(S.lw2, 16)
    V.quantize_mx(T.w2q[:], T.w2s[:], T.w2t[:]).then_inc(S.qw2, 1)
    for c in range(NCH):
        V.wait_ge(S["y%d" % c], 1)
        V.tensor_copy(T.yt[:, CW * c:CW * c + CW], ybank[c]).then_inc(S["yc%d" % c], 1)

    for b in range(G):
        A.wait_ge(S["mx0%d" % b], 1)
        A.activation(piece(T.sq, 0, b), z(0, b), Act.Square, scale=RS, accum_out=share(b)).then_inc(S["sqd%d" % b], 1)
    A.wait_ge(S.bi0, 1)
    A.wait_ge(S["sqd%d" % (G - 1)], 1)
    A.activation(col(T.rt, 0), share(G - 1), Act.Sqrt, bias=T.bi[:, 0:1]).then_inc(S.rt0, 1)
    A.wait_ge(S.rq0, 1)
    A.wait_ge(S.rt0, 1)
    A.activation(col(T.sc, 0), col(T.rt, 0), Act.Copy, scale=rq0).then_inc(S.r0, 1)
    A.wait_ge(S.r0, 1)
    scale(A, 0, 1)
    scale(A, 0, 3)
    A.wait_ge(S.mx1a, 1)
    A.activation(T.sq[:, 512:768], zA, Act.Square, scale=RS, accum_out=T.a1[:, 0:1]).then_inc(S.s1a, 1)
    A.wait_ge(S.mx1b, 1)
    A.activation(T.sq[:, 768:1024], zB, Act.Square, scale=RS, accum_out=T.a1[:, 2:3]).then_inc(S.s1b, 1)
    A.wait_ge(S.s1a, 1)
    A.activation(T.a1[:, 1:2], T.a1[:, 0:1], Act.Identity, bias=EPS).then_inc(S.s1e, 1)
    A.wait_ge(S.s1b, 1)
    A.wait_ge(S.s1e, 1)
    A.activation(col(T.rt, 1), T.a1[:, 2:3], Act.Sqrt, bias=T.a1[:, 1:2]).then_inc(S.rt1, 1)
    A.wait_ge(S.r1, 1)
    scale(A, 1, 2)
    scale(A, 1, 3)
    into_tile(A, 1, 2)
    into_tile(A, 1, 3)

    P.wait_ge(S.qx0, 1)
    for b in range(G):
        P.wait_ge(S["qw1_%d" % b], 1)
        P.matmul_mx(z(0, b), T.xq[:, 0:CW], T.xs[:, 0:CW],
                    T.w1q[:, CW * b:CW * b + CW], T.w1s[:, CW * b:CW * b + CW], True, True).then_inc(S["mx0%d" % b], 1)
    P.wait_ge(S.qx1, 1)
    P.matmul_mx(zA, T.xq[:, CW:2 * CW], T.xs[:, CW:2 * CW], T.w1q[:, 0:256], T.w1s[:, 0:256], True, True).then_inc(S.mx1a, 1)
    P.matmul_mx(zB, T.xq[:, CW:2 * CW], T.xs[:, CW:2 * CW], T.w1q[:, 256:512], T.w1s[:, 256:512], True, True).then_inc(S.mx1b, 1)
    P.wait_ge(S.idb, 1)

    def turn(c, b):
        P.wait_ge(S["sc%d%d" % (c, b)], 1)
        P.matmul(z(c, b), piece(T.rb, c, b), T.identb[:], True, True).then_inc(S["tr%d%d" % (c, b)], 1)

    for b in range(G):
        P.wait_ge(S["sqd%d" % b], 1)
        turn(0, b)
    P.wait_ge(S.mu0, G)
    for b in (0, 2, 1, 3):
        turn(1, b)
    P.wait_ge(S.qw2, 1)
    for c in range(NCH):
        P.wait_ge(S["qh%d" % c], 1)
        P.matmul_mx(ybank[c], T.w2q[:, 0:CW], T.w2s[:, 0:CW],
                    T.hq[:, CW * c:CW * c + CW], T.hs[:, CW * c:CW * c + CW], True, False)
    inc = _route(T, topo, (rank + 1) % n)
    landed = _engines(topo.mask(inc[2], core)) + _engines(topo.mask(inc[3], core))
    for c in range(NCH):
        P.wait_ge(S["arr%d" % c], landed)
        P.matmul_mx(ybank[c], T.w2q[:, CW:2 * CW], T.w2s[:, CW:2 * CW],
                    T.rq[:, CW * c:CW * c + CW], T.rs[:, CW * c:CW * c + CW], False, True).then_inc(S["y%d" % c], 1)

    out = _route(T, topo, rank)
    left = 0
    for c in range(NCH):
        via_q, via_s = _via(out, c)
        to_q = out[1] if via_q == core else via_q
        to_s = out[1] if via_s == core else via_s
        g.wait_ge(S["qh%d" % c], 1)
        left += _send(g, T, topo, core, to_q, _codes(T.rq, c), _codes(T.hq, c), S["arr%d" % c])
        left += _send(g, T, topo, core, to_s, _plane(T.rs, c), _plane(T.hs, c), S["arr%d" % c])
    g.wait_ge(S.sent, left)

    Y.wait_ge(S.mu0, G)
    Y.wait_ge(S.mu1, G)
    Y.wait_ge(S.sent, left)
    Y.dma_start(T.h[:], T.ht[:]).then_inc(S.sh, 16)
    for c in range(NCH):
        Y.wait_ge(S["yc%d" % c], 1)
        Y.dma_start(T.y[:, CW * c:CW * c + CW], T.yt[:, CW * c:CW * c + CW]).then_inc(S["sy%d" % c], 16)
    Y.wait_ge(S.sh, 16)
    for c in range(NCH):
        Y.wait_ge(S["sy%d" % c], 16)
